import numpy as np, ml_dtypes
CORES = [65,73,81,89,97,105,113,121]
N = 8
DEG, TK, TIMES = 3, 128, 2
MASK = [[4,6,0],[4,6,1],[4,6,2],[4,6,3],[4,6,0],[4,6,5],[4,6,0],[4,6,7]]
def setup_inputs(rng):
    return {"x": rng.standard_normal((N, 128, TK), dtype=np.float32).astype(ml_dtypes.bfloat16), "w": (rng.standard_normal((N, 128, DEG * 128), dtype=np.float32) / np.float32(np.sqrt(128 * DEG / 2))).astype(ml_dtypes.bfloat16)}
def setup_inputs_big(rng):
    d = setup_inputs(rng)
    for k in ("x",): d[k] = (d[k].astype(np.float32) * 1048576.0).astype(d[k].dtype)
    return d
def setup_inputs_small(rng):
    d = setup_inputs(rng)
    for k in ("x",): d[k] = (d[k].astype(np.float32) * (1 / 1048576.0)).astype(d[k].dtype)
    return d
def setup_inputs_apart(rng):
    d = setup_inputs(rng)
    f = (10.0 ** rng.permutation(np.linspace(-1.5, 1.5, N))).astype(np.float32).reshape(N, 1, 1)
    for k in ("x",): d[k] = (d[k].astype(np.float32) * f).astype(d[k].dtype)
    return d
def reference(x, w):
    X, W = x.astype(np.float64), w.astype(np.float64)
    h = list(X)
    for _ in range(TIMES):
        h = [np.maximum(sum(W[r][:, 128 * i:128 * i + 128].T @ h[j] for i, j in enumerate(MASK[r])), 0.0) for r in range(N)]
    return {"y": np.stack(h).astype(ml_dtypes.bfloat16)}

from concourse.bass import DstId, RemoteDMATransfer
from concourse.mybir import AluOpType

TK = 128
DEG = 3
SCRATCH = {
    "xin": ("sbuf", [128, (DEG + 1) * TK], "bfloat16"),
    "hin": ("sbuf", [128, (DEG + 1) * TK], "bfloat16"),
    "wsb": ("sbuf", [128, DEG * TK], "bfloat16"),
    "zero": ("sbuf", [128, TK], "float32"),
    "yout": ("sbuf", [128, TK], "bfloat16"),
    "ps1": ("psum", [128, 512], "float32"),
    "ps2": ("psum", [128, 512], "float32"),
}
SEMAPHORES = (["lx", "lw", "z", "m1", "r1", "m2", "r2", "st", "snt", "aw"]
              + ["ax%d" % i for i in range(DEG + 1)] + ["ah%d" % i for i in range(DEG + 1)])


def _bits(m):
    return bin(m).count("1")


def _plan(T, topo):
    mask = T.tables["MASK"]
    cores = list(T.cores)
    n = len(cores)
    every = list(range(topo.CHIPS * topo.CORES_PER_CHIP))
    cons = [[r for r in range(n) if r != j and j in mask[r]] for j in range(n)]
    hubs = [j for j in range(n) if cons[j]]
    far = {j: [r for r in cons[j] if not topo.may_write(cores[j], cores[r])] for j in hubs}
    near = {j: [r for r in cons[j] if r not in far[j]] for j in hubs}
    sends = {}
    expect = {}

    def own_slot(r):
        return mask[r].index(r) if r in mask[r] else DEG

    def anywhere(c):
        m = -1
        for d in every:
            if d != c:
                m &= topo.mask(c, d)
        return m

    def add(core, wait, kind, src_slot, dests, m):
        run = []
        for d in list(dests) + [None]:
            if run and (d is None or d[1] != run[0][1]):
                sem = "aw" if kind == "w" else "a%s%d" % (kind, run[0][1])
                sends.setdefault(core, []).append((wait, kind, src_slot, run, sem, m))
                for dc, _s in run:
                    expect[(dc, sem)] = expect.get((dc, sem), 0) + _bits(m)
                run = []
            if d is not None:
                run.append(d)

    twin = {}
    relays = {}
    for j in hubs:
        if far[j]:
            src = cores[j]
            free = [c for c in every if topo.chip(c) == topo.chip(src) and c not in cores
                    and all(topo.may_write(c, cores[r]) for r in cons[j])]
            same = [c for c in free if topo.die(c) == topo.die(src)]
            other = [c for c in free if topo.die(c) != topo.die(src)]
            twin[j] = same[0]
            relays[j] = other + same[1:]
    with_twin = [j for j in hubs if j in twin]

    for j in hubs:
        src = cores[j]
        out = anywhere(src)
        s = own_slot(j)
        first = [(twin[k], mask[k].index(j)) for k in ([j] if j in twin else []) + [k for k in with_twin if k != j]
                 if j in mask[k]]
        direct = sorted([r for r in near[j] if r in hubs or j not in twin], key=lambda r: -len(near.get(r, [])))
        add(src, "lx", "x", s, first + [(cores[r], mask[r].index(j)) for r in direct], out)
        if j in twin:
            k = with_twin.index(j)
            rot = (k * len(far[j])) // len(with_twin)
            order = far[j][rot:] + far[j][:rot]
            via = order + [r for r in near[j] if r not in direct]
            stay = topo.mask(src, twin[j]) & ~out
            add(src, "lw", "w", 0, [(twin[j], 0)], stay)
            groups = [via[a:a + 2] for a in range(1, len(via), 2)]
            feed = [(relays[j][q], mask[grp[0]].index(j)) for q, grp in enumerate(groups)]
            add(src, "lx", "x", s, feed, stay)
            ts = mask[j].index(j) if j in mask[j] else None
            add(twin[j], "ax%d" % ts, "x", ts, [(cores[via[0]], mask[via[0]].index(j))], anywhere(twin[j]))
            for (qc, qs), grp in zip(feed, groups):
                add(qc, "ax%d" % qs, "x", qs, [(cores[r], mask[r].index(j)) for r in grp], anywhere(qc))
            add(twin[j], "r1", "h", DEG, [(cores[r], mask[r].index(j)) for r in order], anywhere(twin[j]))
        hh = sorted([r for r in near[j] if r in hubs], key=lambda r: -len(near[r]))
        rest = [r for r in near[j] if r not in hubs]
        tail = hh[1:] + rest
        if hubs.index(j) % 2:
            tail = tail[::-1]
        add(src, "r1", "h", s, [(cores[r], mask[r].index(j)) for r in hh[:1] + tail], out)
    return sends, expect, {twin[j]: j for j in twin}


def _slot(buf, i):
    return buf[:, i * TK:(i + 1) * TK]


def rank_program(g, core, T, topo):
    sends, expect, twin_of = _plan(T, topo)
    rank = T.rank_of(core)
    model = rank if rank is not None else twin_of.get(core)
    mask = T.tables["MASK"]
    sem = T.sem

    if rank is not None:
        own = mask[rank].index(rank) if rank in mask[rank] else DEG
        g.sync.dma_start(out=_slot(T.xin, own), in_=T.x[:, :]).then_inc(sem.lx, 16)
        g.scalar.dma_start(out=T.wsb[:, :], in_=T.w[:, :]).then_inc(sem.lw, 16)
    else:
        own = DEG

    total = 0
    for wait, kind, src_slot, dests, asem, m in sends.get(core, []):
        if wait in ("lx", "lw"):
            g.wait_ge(sem[wait], 16)
        elif wait == "r1":
            g.wait_ge(sem.r1, 1)
        else:
            g.wait_ge(sem[wait], expect[(core, wait)])
        if kind == "w":
            src, dsts = T.wsb[:, :], [T.wsb[:, :] for _d in dests]
        else:
            buf = T.xin if kind == "x" else T.hin
            src, dsts = _slot(buf, src_slot), [_slot(buf, ds) for _c, ds in dests]
        ids = []
        for dc, _s in dests:
            rid, pid, _se = topo.addr(dc)
            ids.append(DstId(rid=rid, pnc=pid))
        g.remote_dma_fused([RemoteDMATransfer(dst_ids=ids, dma_engine_mask=m, remote_sem=sem[asem],
                                              srcs=[src], dsts=dsts, alu_op=0)], local_sem=sem.snt)
        total += _bits(m)
    if total:
        g.wait_ge(sem.snt, total)

    if model is None:
        return

    te, ve = g.tensor, g.vector
    ve.memset(T.zero[:, :], 0.0).then_inc(sem.z, 1)
    ve.wait_ge(sem.z, 1)
    home = [i for i in range(DEG) if mask[model][i] == model]
    order = home + [i for i in range(DEG) if i not in home]

    if rank is not None:
        te.wait_ge(sem.lw, 16)
    else:
        te.wait_ge(sem.aw, expect[(core, "aw")])
    for n, i in enumerate(order):
        if rank is not None and i in home:
            te.wait_ge(sem.lx, 16)
        else:
            te.wait_ge(sem["ax%d" % i], expect[(core, "ax%d" % i)])
        mm = te.matmul(out=T.ps1[:, 0:TK], lhsT=_slot(T.wsb, i), rhs=_slot(T.xin, i),
                       start=(n == 0), stop=(n == DEG - 1))
    mm.then_inc(sem.m1, 1)
    ve.wait_ge(sem.m1, 1)
    ve.tensor_tensor(out=_slot(T.hin, own), in0=T.ps1[:, 0:TK], in1=T.zero[:, :], op=AluOpType.max).then_inc(sem.r1, 1)
    if rank is None:
        return

    for n, i in enumerate(order):
        if i in home:
            te.wait_ge(sem.r1, 1)
        else:
            te.wait_ge(sem["ah%d" % i], expect[(core, "ah%d" % i)])
        mm = te.matmul(out=T.ps2[:, 0:TK], lhsT=_slot(T.wsb, i), rhs=_slot(T.hin, i),
                       start=(n == 0), stop=(n == DEG - 1))
    mm.then_inc(sem.m2, 1)
    ve.wait_ge(sem.m2, 1)
    ve.tensor_tensor(out=T.yout[:, :], in0=T.ps2[:, 0:TK], in1=T.zero[:, :], op=AluOpType.max).then_inc(sem.r2, 1)
    g.sync.wait_ge(sem.r2, 1)
    g.sync.dma_start(out=T.y[:, :], in_=T.yout[:, :]).then_inc(sem.st, 16)
    g.sync.wait_ge(sem.st, 16)
